import numpy as np
import ml_dtypes


def mxq(x, axis, fmt="e4m3"):
    dtype, down = {"e4m3": (ml_dtypes.float8_e4m3fn, 7), "e5m2": (ml_dtypes.float8_e5m2, 14)}[fmt]
    v = np.moveaxis(np.asarray(x, np.float32).astype(ml_dtypes.bfloat16).astype(np.float64), axis, -1)
    blocks = v.reshape(v.shape[:-1] + (-1, 32))
    amax = np.abs(blocks).max(-1, keepdims=True)
    byte = np.maximum(np.where(amax > 0, np.frexp(amax)[1] - 1 + 127, 0) - down, 1)
    scale = np.exp2(byte - 127.0)
    codes = (blocks / scale).astype(np.float32).astype(dtype).astype(np.float64)
    return np.moveaxis((codes * scale).reshape(v.shape), -1, axis)


WIDE = False


def mx_kscale(k):
    if not WIDE:
        return np.ones(k)
    levels = np.array([30, -30])
    if k % 512:
        return np.exp2(np.random.permutation(np.resize(levels, k // 32))).repeat(32)
    a = np.empty((k // 512, 16))
    for p in range(k // 512):
        a[p, :8] = np.random.permutation(np.resize(levels, 8))
        for g in range(8):
            far = levels[np.abs(levels - a[p, g]) >= 10]
            a[p, g + 8] = far[np.random.randint(len(far))]
    return np.exp2(a.ravel()).repeat(32)


def f64(x):
    return np.asarray(x).astype(np.float64)


def striped(idx):
    return np.tile(idx.reshape(-1, 16).T, (8, 1)).astype(np.uint16)


def unstriped(offs):
    return offs[:16].T.reshape(-1).astype(np.int64)


K, T, E, C, N = 256, 2048, 4, 512, 512


def setup_inputs():
    n = np.random.standard_normal
    idx = np.random.permutation(T)[:E * C]
    s = mx_kscale(E * C)[None, :]
    xT = n((K, T)); dyT = n((N, T))
    xT[:, idx] *= s; dyT[:, idx] /= s
    return {
        "xT": xT.astype(np.float32),
        "dyT": dyT.astype(np.float32),
        "gate": np.tile(np.random.uniform(0.2, 1.0, E * C), (N, 1)).astype(np.float32),
        "offs": striped(idx),
    }


def reference(xT, dyT, gate, offs):
    idx = unstriped(offs)
    xq = mxq(f64(xT)[:, idx], 1, "e4m3")
    gq = mxq(f64(gate) * f64(dyT)[:, idx], 1, "e5m2")
    return np.stack([(xq[:, e * C:(e + 1) * C] @ gq[:, e * C:(e + 1) * C].T) for e in range(E)])

@@ -1,0 +1,131 @@
+from contextlib import ExitStack
+
+import concourse.mybir as mybir
+from concourse.masks import make_identity
+
+K, T, E, C, N = 256, 2048, 4, 512, 512
+P = 128
+FLOPS = 2 * E * C * K * N
+BYTES = 4 * (K * T + N * T + E * C + E * K * N) + 2 * E * C
+
+F32 = mybir.dt.float32
+BF16 = mybir.dt.bfloat16
+U32 = mybir.dt.uint32
+U16 = mybir.dt.uint16
+U8 = mybir.dt.uint8
+E4M3 = mybir.dt.float8_e4m3fn_x4
+E5M2 = mybir.dt.float8_e5m2_x4
+MULT = mybir.AluOpType.mult
+COPY = mybir.ActivationFunctionType.Copy
+
+KB = K // P
+NB = N // P
+OC = C // 16
+
+
+def tile_moe_bdw_lin_none_kernel(tc, xT, dyT, gate, offs, out):
+    nc = tc.nc
+    with ExitStack() as ctx:
+        held = ctx.enter_context(tc.tile_pool(name="held", bufs=1))
+        work = ctx.enter_context(tc.tile_pool(name="work", bufs=1))
+        psum = ctx.enter_context(tc.psum_pool(name="psum", bufs=1))
+
+        offsets = held.tile([P, E * OC], U16, name="offsets")
+        nc.sync.dma_start(offsets[:], offs)
+
+        gates = held.tile([P, E * C], F32, name="gates")
+        dy = [held.tile([P, T], F32, name=f"dy{b}") for b in range(NB)]
+        x32 = [held.tile([P, T], F32, name=f"x32_{b}") for b in range(KB)]
+        x16 = [held.tile([P, T], BF16, name=f"x16_{b}", align_bytes=64) for b in range(KB)]
+
+        def load_gate(a, b):
+            nc.sync.dma_start(gates[:, a * C : b * C], gate[0:P, a * C : b * C])
+
+        def load_dy(b):
+            nc.sync.dma_start(dy[b][:], dyT[b * P : (b + 1) * P, :])
+
+        def load_x(b):
+            nc.sync.dma_start(x32[b][:], xT[b * P : (b + 1) * P, :])
+
+        load_gate(0, 1)
+        load_dy(0)
+        load_x(0)
+        load_gate(1, E)
+        load_dy(1)
+        load_x(1)
+        load_dy(2)
+        load_dy(3)
+
+        ident = held.tile([P, P], F32, name="ident")
+        make_identity(nc, ident[:])
+
+        g16 = [work.tile([P, N, 4], BF16, name=f"g16_{e}", align_bytes=64) for e in range(E)]
+        xs16 = [work.tile([P, K, 4], BF16, name=f"xs16_{e}", align_bytes=64) for e in range(E)]
+        xpicked = {}
+
+        def part(e):
+            return offsets[:, e * OC : (e + 1) * OC]
+
+        def grad(b, e):
+            picked = work.tile([P, C], F32, name="picked", bufs=6)
+            nc.vector.tensor_tensor(picked[:], dy[b][:].indirect(part(e)), gates[:, e * C : (e + 1) * C], MULT)
+            bank = psum.tile([P, 4, P], F32, name="turned", bufs=5)
+            for t in range(4):
+                nc.tensor.transpose(bank[:, t, :], picked[:, t:C:4], ident[:])
+            nc.scalar.copy(out=g16[e][:, b * P : (b + 1) * P, :], in_=bank[:].rearrange("p t n -> p n t"))
+
+        def cast(b):
+            nc.vector.tensor_copy(out=x16[b][:], in_=x32[b][:])
+
+        def token(b, e):
+            picked = work.tile([P, 2, P, 2], BF16, name="xpicked", bufs=8, align_bytes=64)
+            nc.scalar.activation(picked[:].rearrange("p u i s -> p i u s"), x16[b][:].indirect(part(e)), COPY)
+            xpicked[b, e] = picked
+
+        def turn(e):
+            bank = psum.tile([P, 2, K], F32, name="turned", bufs=5)
+            for b in range(KB):
+                words = xpicked[b, e][:].rearrange("p u i s -> p (u i s)").bitcast(F32)
+                for u in range(2):
+                    nc.tensor.transpose(bank[:, u, b * P : (b + 1) * P], words[:, u * P : (u + 1) * P], ident[:])
+            nc.scalar.copy(
+                out=xs16[e][:].rearrange("p k t -> p (k t)").bitcast(F32).rearrange("p (k u) -> p k u", u=2),
+                in_=bank[:].rearrange("p u k -> p k u"),
+            )
+
+        def product(e):
+            xc = work.tile([P, K], U32, name=f"xc{e}", align_bytes=64)
+            xsc = work.tile([P, K], U8, name=f"xsc{e}", align_bytes=64)
+            nc.vector.quantize_mx(out=xc[:].bitcast(E4M3), scales=xsc[:], in_=xs16[e][:].rearrange("p k t -> p (k t)"))
+            gc = work.tile([P, N], U32, name=f"gc{e}", align_bytes=64)
+            gsc = work.tile([P, N], U8, name=f"gsc{e}", align_bytes=64)
+            nc.vector.quantize_mx(out=gc[:].bitcast(E5M2), scales=gsc[:], in_=g16[e][:].rearrange("p n t -> p (n t)"))
+            for b in range(KB):
+                cols = slice(b * P, (b + 1) * P)
+                acc = psum.tile([P, N], F32, name="acc", bufs=3)
+                nc.tensor.matmul_mx(
+                    out=acc[:], lhsT=xc[:, cols].bitcast(E4M3), lhsT_scale=xsc[:, cols],
+                    rhs=gc[:].bitcast(E5M2), rhs_scale=gsc[:], start=True, stop=True,
+                )
+                res = work.tile([P, N], F32, name="res", bufs=4)
+                if b == 0:
+                    nc.scalar.copy(out=res[:], in_=acc[:])
+                else:
+                    nc.vector.tensor_copy(out=res[:], in_=acc[:])
+                nc.sync.dma_start(out[e, cols, :], res[:])
+
+        grad(0, 0)
+        cast(0)
+        for e in range(1, E):
+            grad(0, e)
+        for e in range(E):
+            token(0, e)
+            grad(1, e)
+        cast(1)
+        for e in range(E):
+            token(1, e)
+            grad(2, e)
+        for e in range(E):
+            turn(e)
+            grad(3, e)
+            product(e)

@@ -4,7 +4,6 @@ import concourse.mybir as mybir
 from concourse.masks import make_identity
 
 K, T, E, C, N = 256, 2048, 4, 512, 512
-P = 128
 FLOPS = 2 * E * C * K * N
 BYTES = 4 * (K * T + N * T + E * C + E * K * N) + 2 * E * C
 
@@ -18,9 +17,13 @@ E5M2 = mybir.dt.float8_e5m2_x4
 MULT = mybir.AluOpType.mult
 COPY = mybir.ActivationFunctionType.Copy
 
+P = 128
+PACK = 4
 KB = K // P
 NB = N // P
-OC = C // 16
+COLS = C // 16
+PAIRS = ((0, 1), (2, 3))
+SHARE = 512
 
 
 def tile_moe_bdw_lin_none_kernel(tc, xT, dyT, gate, offs, out):
@@ -30,102 +33,148 @@ def tile_moe_bdw_lin_none_kernel(tc, xT, dyT, gate, offs, out):
         work = ctx.enter_context(tc.tile_pool(name="work", bufs=1))
         psum = ctx.enter_context(tc.psum_pool(name="psum", bufs=1))
 
-        offsets = held.tile([P, E * OC], U16, name="offsets")
+        offsets = held.tile([P, E * COLS], U16, name="offsets")
         nc.sync.dma_start(offsets[:], offs)
 
         gates = held.tile([P, E * C], F32, name="gates")
         dy = [held.tile([P, T], F32, name=f"dy{b}") for b in range(NB)]
         x32 = [held.tile([P, T], F32, name=f"x32_{b}") for b in range(KB)]
         x16 = [held.tile([P, T], BF16, name=f"x16_{b}", align_bytes=64) for b in range(KB)]
+        ident = held.tile([P, P], F32, name="ident")
+        make_identity(nc, ident[:])
 
-        def load_gate(a, b):
-            nc.sync.dma_start(gates[:, a * C : b * C], gate[0:P, a * C : b * C])
+        def load_x(b, lo, hi):
+            nc.sync.dma_start(x32[b][:, lo:hi], xT[b * P : (b + 1) * P, lo:hi])
 
         def load_dy(b):
             nc.sync.dma_start(dy[b][:], dyT[b * P : (b + 1) * P, :])
 
-        def load_x(b):
-            nc.sync.dma_start(x32[b][:], xT[b * P : (b + 1) * P, :])
+        def load_gates(e0, e1):
+            nc.sync.dma_start(gates[:, e0 * C : e1 * C], gate[0:P, e0 * C : e1 * C])
 
-        load_gate(0, 1)
+        CUTS = ((0, T // 2), (T // 2, 3 * T // 4), (3 * T // 4, T))
+        for lo, hi in CUTS:
+            load_x(0, lo, hi)
+        load_gates(0, 1)
         load_dy(0)
-        load_x(0)
-        load_gate(1, E)
+        load_gates(1, 2)
+        load_gates(2, E)
+        load_x(1, 0, T)
         load_dy(1)
-        load_x(1)
         load_dy(2)
         load_dy(3)
 
-        ident = held.tile([P, P], F32, name="ident")
-        make_identity(nc, ident[:])
+        g_bf16 = [work.tile([P, N, PACK], BF16, name=f"g_bf16_{e}", align_bytes=64) for e in range(E)]
+        x2_bf16 = [work.tile([P, 2, K, PACK], BF16, name=f"x2_bf16_{h}", align_bytes=64) for h in range(2)]
+        x_codes = [work.tile([P, 2, K], U32, name=f"x_codes{h}", align_bytes=64) for h in range(2)]
+        x_scales = [work.tile([P, 2, K], U8, name=f"x_scales{h}", align_bytes=64) for h in range(2)]
+        g_codes = [work.tile([P, N], U32, name=f"g_codes{e}", align_bytes=64) for e in range(E)]
+        g_scales = [work.tile([P, N], U8, name=f"g_scales{e}", align_bytes=64) for e in range(E)]
+        x_picked, g_picked = {}, {}
 
-        g16 = [work.tile([P, N, 4], BF16, name=f"g16_{e}", align_bytes=64) for e in range(E)]
-        xs16 = [work.tile([P, K, 4], BF16, name=f"xs16_{e}", align_bytes=64) for e in range(E)]
-        xpicked = {}
+        def slots(es):
+            return offsets[:, es[0] * COLS : (es[-1] + 1) * COLS]
 
-        def part(e):
-            return offsets[:, e * OC : (e + 1) * OC]
+        def gather_g(b, es):
+            picked = work.tile([P, len(es) * C], F32, name="picked", bufs=5)
+            nc.vector.tensor_tensor(
+                picked[:], dy[b][:].indirect(slots(es)), gates[:, es[0] * C : (es[-1] + 1) * C], MULT
+            )
+            for e in es:
+                g_picked[b, e] = picked[:, (e - es[0]) * C : (e - es[0] + 1) * C]
 
-        def grad(b, e):
-            picked = work.tile([P, C], F32, name="picked", bufs=6)
-            nc.vector.tensor_tensor(picked[:], dy[b][:].indirect(part(e)), gates[:, e * C : (e + 1) * C], MULT)
-            bank = psum.tile([P, 4, P], F32, name="turned", bufs=5)
-            for t in range(4):
-                nc.tensor.transpose(bank[:, t, :], picked[:, t:C:4], ident[:])
-            nc.scalar.copy(out=g16[e][:, b * P : (b + 1) * P, :], in_=bank[:].rearrange("p t n -> p n t"))
+        def turn_g(b, e):
+            bank = psum.tile([P, PACK, P], F32, name="turned", bufs=5)
+            for t in range(PACK):
+                nc.tensor.transpose(bank[:, t, :], g_picked[b, e][:, t:C:PACK], ident[:])
+            nc.scalar.copy(out=g_bf16[e][:, b * P : (b + 1) * P, :], in_=bank[:].rearrange("p t n -> p n t"))
 
-        def cast(b):
-            nc.vector.tensor_copy(out=x16[b][:], in_=x32[b][:])
+        def gather_x(b, h):
+            picked = work.tile([P, 2, 2 * P, 2], BF16, name=f"x_picked{b}_{h}", align_bytes=64)
+            nc.scalar.activation(picked[:].rearrange("p u i s -> p i u s"), x16[b][:].indirect(slots(PAIRS[h])), COPY)
+            x_picked[b, h] = picked
 
-        def token(b, e):
-            picked = work.tile([P, 2, P, 2], BF16, name="xpicked", bufs=8, align_bytes=64)
-            nc.scalar.activation(picked[:].rearrange("p u i s -> p i u s"), x16[b][:].indirect(part(e)), COPY)
-            xpicked[b, e] = picked
-
-        def turn(e):
+        def turn_x(e):
+            h, i = divmod(e, 2)
             bank = psum.tile([P, 2, K], F32, name="turned", bufs=5)
             for b in range(KB):
-                words = xpicked[b, e][:].rearrange("p u i s -> p (u i s)").bitcast(F32)
+                words = x_picked[b, h][:].rearrange("p u i s -> p (u i s)").bitcast(F32)
                 for u in range(2):
-                    nc.tensor.transpose(bank[:, u, b * P : (b + 1) * P], words[:, u * P : (u + 1) * P], ident[:])
+                    lo = (2 * u + i) * P
+                    nc.tensor.transpose(bank[:, u, b * P : (b + 1) * P], words[:, lo : lo + P], ident[:])
+            words = x2_bf16[h][:].rearrange("p e k t -> p (e k t)").bitcast(F32)
             nc.scalar.copy(
-                out=xs16[e][:].rearrange("p k t -> p (k t)").bitcast(F32).rearrange("p (k u) -> p k u", u=2),
+                out=words[:, i * 2 * K : (i + 1) * 2 * K].rearrange("p (k u) -> p k u", u=2),
                 in_=bank[:].rearrange("p u k -> p k u"),
             )
 
-        def product(e):
-            xc = work.tile([P, K], U32, name=f"xc{e}", align_bytes=64)
-            xsc = work.tile([P, K], U8, name=f"xsc{e}", align_bytes=64)
-            nc.vector.quantize_mx(out=xc[:].bitcast(E4M3), scales=xsc[:], in_=xs16[e][:].rearrange("p k t -> p (k t)"))
-            gc = work.tile([P, N], U32, name=f"gc{e}", align_bytes=64)
-            gsc = work.tile([P, N], U8, name=f"gsc{e}", align_bytes=64)
-            nc.vector.quantize_mx(out=gc[:].bitcast(E5M2), scales=gsc[:], in_=g16[e][:].rearrange("p n t -> p (n t)"))
+        def quantize_x(h):
+            nc.vector.quantize_mx(
+                out=x_codes[h][:].rearrange("p e k -> p (e k)").bitcast(E4M3),
+                scales=x_scales[h][:].rearrange("p e k -> p (e k)"),
+                in_=x2_bf16[h][:].rearrange("p e k t -> p (e k t)"),
+            )
+
+        def quantize_g(e, b0, b1):
+            cols = slice(b0 * P, b1 * P)
+            nc.vector.quantize_mx(
+                out=g_codes[e][:, cols].bitcast(E5M2),
+                scales=g_scales[e][:, cols],
+                in_=g_bf16[e][:, cols, :].rearrange("p n t -> p (n t)"),
+            )
+
+        def multiply(e, engines):
+            h, i = divmod(e, 2)
             for b in range(KB):
                 cols = slice(b * P, (b + 1) * P)
-                acc = psum.tile([P, N], F32, name="acc", bufs=3)
+                total = psum.tile([P, N], F32, name="total", bufs=3)
                 nc.tensor.matmul_mx(
-                    out=acc[:], lhsT=xc[:, cols].bitcast(E4M3), lhsT_scale=xsc[:, cols],
-                    rhs=gc[:].bitcast(E5M2), rhs_scale=gsc[:], start=True, stop=True,
+                    out=total[:],
+                    lhsT=x_codes[h][:, i, cols].bitcast(E4M3),
+                    lhsT_scale=x_scales[h][:, i, cols],
+                    rhs=g_codes[e][:].bitcast(E5M2),
+                    rhs_scale=g_scales[e][:],
+                    start=True,
+                    stop=True,
                 )
-                res = work.tile([P, N], F32, name="res", bufs=4)
-                if b == 0:
-                    nc.scalar.copy(out=res[:], in_=acc[:])
+                result = work.tile([P, N], F32, name="result", bufs=4)
+                if engines[b] == "S":
+                    nc.scalar.copy(out=result[:], in_=total[:])
                 else:
-                    nc.vector.tensor_copy(out=res[:], in_=acc[:])
-                nc.sync.dma_start(out[e, cols, :], res[:])
+                    nc.vector.tensor_copy(out=result[:], in_=total[:])
+                nc.sync.dma_start(out[e, cols, :], result[:])
 
-        grad(0, 0)
-        cast(0)
-        for e in range(1, E):
-            grad(0, e)
+        for lo, hi in CUTS:
+            nc.vector.tensor_copy(out=x16[0][:, lo:hi], in_=x32[0][:, lo:hi])
+        for h in range(2):
+            gather_x(0, h)
+        gather_g(0, (0,))
+        gather_g(0, (1,))
+        turn_g(0, 0)
+        gather_g(0, (2, 3))
+        nc.vector.tensor_copy(out=x16[1][:, 0:SHARE], in_=x32[1][:, 0:SHARE])
+        nc.scalar.copy(out=x16[1][:, SHARE:T], in_=x32[1][:, SHARE:T])
+        turn_g(0, 1)
+        for h in range(2):
+            gather_x(1, h)
+        waiting = (0, (2, 3))
+        step = 0
+        for b in range(1, NB):
+            for es in PAIRS:
+                gather_g(b, es)
+                for e in waiting[1]:
+                    turn_g(waiting[0], e)
+                if 2 <= step < 2 + E:
+                    turn_x(step - 2)
+                step += 1
+                waiting = (b, es)
+        for e in waiting[1]:
+            turn_g(waiting[0], e)
+        quantize_x(0)
+        quantize_g(0, 0, NB)
+        quantize_g(1, 0, NB)
+        quantize_x(1)
+        quantize_g(2, 0, NB)
+        quantize_g(3, 0, NB)
         for e in range(E):
-            token(0, e)
-            grad(1, e)
-        cast(1)
-        for e in range(E):
-            token(1, e)
-            grad(2, e)
-        for e in range(E):
-            turn(e)
-            grad(3, e)
-            product(e)
+            multiply(e, "SS" if e == 0 else "SV")

@@ -23,7 +23,8 @@ KB = K // P
 NB = N // P
 COLS = C // 16
 PAIRS = ((0, 1), (2, 3))
-SHARE = 512
+ROWS = 2 * C // P
+SHARE = 1024
 
 
 def tile_moe_bdw_lin_none_kernel(tc, xT, dyT, gate, offs, out):
@@ -36,7 +37,8 @@ def tile_moe_bdw_lin_none_kernel(tc, xT, dyT, gate, offs, out):
         offsets = held.tile([P, E * COLS], U16, name="offsets")
         nc.sync.dma_start(offsets[:], offs)
 
-        gates = held.tile([P, E * C], F32, name="gates")
+        gates = [held.tile([P, 2 * C], F32, name=f"gates{h}") for h in range(2)]
+        gate_cols = held.tile([P, ROWS], F32, name="gate_cols")
         dy = [held.tile([P, T], F32, name=f"dy{b}") for b in range(NB)]
         x32 = [held.tile([P, T], F32, name=f"x32_{b}") for b in range(KB)]
         x16 = [held.tile([P, T], BF16, name=f"x16_{b}", align_bytes=64) for b in range(KB)]
@@ -49,16 +51,13 @@ def tile_moe_bdw_lin_none_kernel(tc, xT, dyT, gate, offs, out):
         def load_dy(b):
             nc.sync.dma_start(dy[b][:], dyT[b * P : (b + 1) * P, :])
 
-        def load_gates(e0, e1):
-            nc.sync.dma_start(gates[:, e0 * C : e1 * C], gate[0:P, e0 * C : e1 * C])
 
+        nc.sync.dma_start(gate_cols[:], gate[0:1, 0 : 2 * C].rearrange("o (p c) -> (o p) c", c=ROWS))
         CUTS = ((0, T // 2), (T // 2, 3 * T // 4), (3 * T // 4, T))
         for lo, hi in CUTS:
             load_x(0, lo, hi)
-        load_gates(0, 1)
         load_dy(0)
-        load_gates(1, 2)
-        load_gates(2, E)
+        nc.sync.dma_start(gates[1][:], gate[0:P, 2 * C : 4 * C])
         load_x(1, 0, T)
         load_dy(1)
         load_dy(2)
@@ -72,13 +71,23 @@ def tile_moe_bdw_lin_none_kernel(tc, xT, dyT, gate, offs, out):
         g_scales = [work.tile([P, N], U8, name=f"g_scales{e}", align_bytes=64) for e in range(E)]
         x_picked, g_picked = {}, {}
 
+        def spread_gate(i):
+            bank = psum.tile([P, PACK, P], F32, name="turned", bufs=5)
+            for j in range(PACK):
+                c = PACK * i + j
+                nc.tensor.transpose(bank[:, j, :], gate_cols[:, c : c + 1].to_broadcast([P, P]), ident[:])
+            nc.vector.tensor_copy(
+                out=gates[0][:].rearrange("q (p c) -> q p c", c=ROWS)[:, :, PACK * i : PACK * (i + 1)],
+                in_=bank[:].rearrange("q c p -> q p c"),
+            )
+
         def slots(es):
             return offsets[:, es[0] * COLS : (es[-1] + 1) * COLS]
 
         def gather_g(b, es):
             picked = work.tile([P, len(es) * C], F32, name="picked", bufs=5)
             nc.vector.tensor_tensor(
-                picked[:], dy[b][:].indirect(slots(es)), gates[:, es[0] * C : (es[-1] + 1) * C], MULT
+                picked[:], dy[b][:].indirect(slots(es)), gates[es[0] // 2][:], MULT
             )
             for e in es:
                 g_picked[b, e] = picked[:, (e - es[0]) * C : (e - es[0] + 1) * C]
@@ -146,28 +155,27 @@ def tile_moe_bdw_lin_none_kernel(tc, xT, dyT, gate, offs, out):
 
         for lo, hi in CUTS:
             nc.vector.tensor_copy(out=x16[0][:, lo:hi], in_=x32[0][:, lo:hi])
+        spread_gate(0)
+        spread_gate(1)
         for h in range(2):
             gather_x(0, h)
-        gather_g(0, (0,))
-        gather_g(0, (1,))
-        turn_g(0, 0)
-        gather_g(0, (2, 3))
-        nc.vector.tensor_copy(out=x16[1][:, 0:SHARE], in_=x32[1][:, 0:SHARE])
-        nc.scalar.copy(out=x16[1][:, SHARE:T], in_=x32[1][:, SHARE:T])
-        turn_g(0, 1)
-        for h in range(2):
-            gather_x(1, h)
-        waiting = (0, (2, 3))
-        step = 0
-        for b in range(1, NB):
-            for es in PAIRS:
-                gather_g(b, es)
+        waiting = None
+        for step in range(2 * NB):
+            b, h = divmod(step, 2)
+            es = PAIRS[h]
+            gather_g(b, es)
+            if waiting:
                 for e in waiting[1]:
                     turn_g(waiting[0], e)
-                if 2 <= step < 2 + E:
-                    turn_x(step - 2)
-                step += 1
-                waiting = (b, es)
+            if step == 1:
+                nc.vector.tensor_copy(out=x16[1][:, 0:SHARE], in_=x32[1][:, 0:SHARE])
+                nc.scalar.copy(out=x16[1][:, SHARE:T], in_=x32[1][:, SHARE:T])
+            if step == 2:
+                gather_x(1, 0)
+                gather_x(1, 1)
+            if 3 <= step < 3 + E:
+                turn_x(step - 3)
+            waiting = (b, es)
         for e in waiting[1]:
             turn_g(waiting[0], e)
         quantize_x(0)

from contextlib import ExitStack

import concourse.mybir as mybir
from concourse.masks import make_identity

K, T, E, C, N = 256, 2048, 4, 512, 512
FLOPS = 2 * E * C * K * N
BYTES = 4 * (K * T + N * T + E * C + E * K * N) + 2 * E * C

F32 = mybir.dt.float32
BF16 = mybir.dt.bfloat16
U32 = mybir.dt.uint32
U16 = mybir.dt.uint16
U8 = mybir.dt.uint8
E4M3 = mybir.dt.float8_e4m3fn_x4
E5M2 = mybir.dt.float8_e5m2_x4
MULT = mybir.AluOpType.mult
COPY = mybir.ActivationFunctionType.Copy

P = 128
PACK = 4
KB = K // P
NB = N // P
COLS = C // 16
PAIRS = ((0, 1), (2, 3))
ROWS = 2 * C // P
SHARE = 1024


def tile_moe_bdw_lin_none_kernel(tc, xT, dyT, gate, offs, out):
    nc = tc.nc
    with ExitStack() as ctx:
        held = ctx.enter_context(tc.tile_pool(name="held", bufs=1))
        work = ctx.enter_context(tc.tile_pool(name="work", bufs=1))
        psum = ctx.enter_context(tc.psum_pool(name="psum", bufs=1))

        offsets = held.tile([P, E * COLS], U16, name="offsets")
        nc.sync.dma_start(offsets[:], offs)

        gates = [held.tile([P, 2 * C], F32, name=f"gates{h}") for h in range(2)]
        gate_cols = held.tile([P, ROWS], F32, name="gate_cols")
        dy = [held.tile([P, T], F32, name=f"dy{b}") for b in range(NB)]
        x32 = [held.tile([P, T], F32, name=f"x32_{b}") for b in range(KB)]
        x16 = [held.tile([P, T], BF16, name=f"x16_{b}", align_bytes=64) for b in range(KB)]
        ident = held.tile([P, P], F32, name="ident")
        make_identity(nc, ident[:])

        def load_x(b, lo, hi):
            nc.sync.dma_start(x32[b][:, lo:hi], xT[b * P : (b + 1) * P, lo:hi])

        def load_dy(b):
            nc.sync.dma_start(dy[b][:], dyT[b * P : (b + 1) * P, :])


        nc.sync.dma_start(gate_cols[:], gate[0:1, 0 : 2 * C].rearrange("o (p c) -> (o p) c", c=ROWS))
        CUTS = ((0, T // 2), (T // 2, 3 * T // 4), (3 * T // 4, T))
        for lo, hi in CUTS:
            load_x(0, lo, hi)
        load_dy(0)
        nc.sync.dma_start(gates[1][:], gate[0:P, 2 * C : 4 * C])
        load_x(1, 0, T)
        load_dy(1)
        load_dy(2)
        load_dy(3)

        g_bf16 = [work.tile([P, N, PACK], BF16, name=f"g_bf16_{e}", align_bytes=64) for e in range(E)]
        x2_bf16 = [work.tile([P, 2, K, PACK], BF16, name=f"x2_bf16_{h}", align_bytes=64) for h in range(2)]
        x_codes = [work.tile([P, 2, K], U32, name=f"x_codes{h}", align_bytes=64) for h in range(2)]
        x_scales = [work.tile([P, 2, K], U8, name=f"x_scales{h}", align_bytes=64) for h in range(2)]
        g_codes = [work.tile([P, N], U32, name=f"g_codes{e}", align_bytes=64) for e in range(E)]
        g_scales = [work.tile([P, N], U8, name=f"g_scales{e}", align_bytes=64) for e in range(E)]
        x_picked, g_picked = {}, {}

        def spread_gate(i):
            bank = psum.tile([P, PACK, P], F32, name="turned", bufs=5)
            for j in range(PACK):
                c = PACK * i + j
                nc.tensor.transpose(bank[:, j, :], gate_cols[:, c : c + 1].to_broadcast([P, P]), ident[:])
            nc.vector.tensor_copy(
                out=gates[0][:].rearrange("q (p c) -> q p c", c=ROWS)[:, :, PACK * i : PACK * (i + 1)],
                in_=bank[:].rearrange("q c p -> q p c"),
            )

        def slots(es):
            return offsets[:, es[0] * COLS : (es[-1] + 1) * COLS]

        def gather_g(b, es):
            picked = work.tile([P, len(es) * C], F32, name="picked", bufs=5)
            nc.vector.tensor_tensor(
                picked[:], dy[b][:].indirect(slots(es)), gates[es[0] // 2][:], MULT
            )
            for e in es:
                g_picked[b, e] = picked[:, (e - es[0]) * C : (e - es[0] + 1) * C]

        def turn_g(b, e):
            bank = psum.tile([P, PACK, P], F32, name="turned", bufs=5)
            for t in range(PACK):
                nc.tensor.transpose(bank[:, t, :], g_picked[b, e][:, t:C:PACK], ident[:])
            nc.scalar.copy(out=g_bf16[e][:, b * P : (b + 1) * P, :], in_=bank[:].rearrange("p t n -> p n t"))

        def gather_x(b, h):
            picked = work.tile([P, 2, 2 * P, 2], BF16, name=f"x_picked{b}_{h}", align_bytes=64)
            nc.scalar.activation(picked[:].rearrange("p u i s -> p i u s"), x16[b][:].indirect(slots(PAIRS[h])), COPY)
            x_picked[b, h] = picked

        def turn_x(e):
            h, i = divmod(e, 2)
            bank = psum.tile([P, 2, K], F32, name="turned", bufs=5)
            for b in range(KB):
                words = x_picked[b, h][:].rearrange("p u i s -> p (u i s)").bitcast(F32)
                for u in range(2):
                    lo = (2 * u + i) * P
                    nc.tensor.transpose(bank[:, u, b * P : (b + 1) * P], words[:, lo : lo + P], ident[:])
            words = x2_bf16[h][:].rearrange("p e k t -> p (e k t)").bitcast(F32)
            nc.scalar.copy(
                out=words[:, i * 2 * K : (i + 1) * 2 * K].rearrange("p (k u) -> p k u", u=2),
                in_=bank[:].rearrange("p u k -> p k u"),
            )

        def quantize_x(h):
            nc.vector.quantize_mx(
                out=x_codes[h][:].rearrange("p e k -> p (e k)").bitcast(E4M3),
                scales=x_scales[h][:].rearrange("p e k -> p (e k)"),
                in_=x2_bf16[h][:].rearrange("p e k t -> p (e k t)"),
            )

        def quantize_g(e, b0, b1):
            cols = slice(b0 * P, b1 * P)
            nc.vector.quantize_mx(
                out=g_codes[e][:, cols].bitcast(E5M2),
                scales=g_scales[e][:, cols],
                in_=g_bf16[e][:, cols, :].rearrange("p n t -> p (n t)"),
            )

        def multiply(e, engines):
            h, i = divmod(e, 2)
            for b in range(KB):
                cols = slice(b * P, (b + 1) * P)
                total = psum.tile([P, N], F32, name="total", bufs=3)
                nc.tensor.matmul_mx(
                    out=total[:],
                    lhsT=x_codes[h][:, i, cols].bitcast(E4M3),
                    lhsT_scale=x_scales[h][:, i, cols],
                    rhs=g_codes[e][:].bitcast(E5M2),
                    rhs_scale=g_scales[e][:],
                    start=True,
                    stop=True,
                )
                result = work.tile([P, N], F32, name="result", bufs=4)
                if engines[b] == "S":
                    nc.scalar.copy(out=result[:], in_=total[:])
                else:
                    nc.vector.tensor_copy(out=result[:], in_=total[:])
                nc.sync.dma_start(out[e, cols, :], result[:])

        for lo, hi in CUTS:
            nc.vector.tensor_copy(out=x16[0][:, lo:hi], in_=x32[0][:, lo:hi])
        spread_gate(0)
        spread_gate(1)
        for h in range(2):
            gather_x(0, h)
        waiting = None
        for step in range(2 * NB):
            b, h = divmod(step, 2)
            es = PAIRS[h]
            gather_g(b, es)
            if waiting:
                for e in waiting[1]:
                    turn_g(waiting[0], e)
            if step == 1:
                nc.vector.tensor_copy(out=x16[1][:, 0:SHARE], in_=x32[1][:, 0:SHARE])
                nc.scalar.copy(out=x16[1][:, SHARE:T], in_=x32[1][:, SHARE:T])
            if step == 2:
                gather_x(1, 0)
                gather_x(1, 1)
            if 3 <= step < 3 + E:
                turn_x(step - 3)
            waiting = (b, es)
        for e in waiting[1]:
            turn_g(waiting[0], e)
        quantize_x(0)
        quantize_g(0, 0, NB)
        quantize_g(1, 0, NB)
        quantize_x(1)
        quantize_g(2, 0, NB)
        quantize_g(3, 0, NB)
        for e in range(E):
            multiply(e, "SS" if e == 0 else "SV")
